import numpy as np
import ml_dtypes


def mxq(x, axis, fmt="e4m3"):
    dtype, down = {"e4m3": (ml_dtypes.float8_e4m3fn, 7), "e5m2": (ml_dtypes.float8_e5m2, 14)}[fmt]
    v = np.moveaxis(np.asarray(x, np.float32).astype(ml_dtypes.bfloat16).astype(np.float64), axis, -1)
    blocks = v.reshape(v.shape[:-1] + (-1, 32))
    amax = np.abs(blocks).max(-1, keepdims=True)
    byte = np.maximum(np.where(amax > 0, np.frexp(amax)[1] - 1 + 127, 0) - down, 1)
    scale = np.exp2(byte - 127.0)
    codes = (blocks / scale).astype(np.float32).astype(dtype).astype(np.float64)
    return np.moveaxis((codes * scale).reshape(v.shape), -1, axis)


WIDE = False


def mx_kscale(k):
    if not WIDE:
        return np.ones(k)
    levels = np.array([10, -10, 5, -5, 0])
    if k % 512:
        return np.exp2(np.random.permutation(np.resize(levels, k // 32))).repeat(32)
    a = np.empty((k // 512, 16))
    for p in range(k // 512):
        a[p, :8] = np.random.permutation(np.resize(levels, 8))
        for g in range(8):
            far = levels[np.abs(levels - a[p, g]) >= 10]
            a[p, g + 8] = far[np.random.randint(len(far))]
    return np.exp2(a.ravel()).repeat(32)


def f64(x):
    return np.asarray(x).astype(np.float64)


def striped(idx):
    return np.tile(np.asarray(idx).reshape(-1, 16).T, (8, 1)).astype(np.uint16)


def unstriped(offs):
    return offs[:16].T.reshape(-1).astype(np.int64)


def striped8(idx):
    return np.asarray(idx).reshape(8, -1, 16).transpose(0, 2, 1).reshape(128, -1).astype(np.uint16)


def unstriped8(offs):
    return offs.reshape(8, 16, -1).transpose(0, 2, 1).reshape(8, -1).astype(np.int64)


def pick8(x, idx, run):
    r = np.arange(len(x))
    return x[r[:, None], idx[r % (8 * run) // run]]


E2M1 = np.array([0.0, 0.5, 1.0, 1.5, 2.0, 3.0, 4.0, 6.0, -0.0, -0.5, -1.0, -1.5, -2.0, -3.0, -4.0, -6.0])


def pack_weight(w, fmt):
    k, n = w.shape
    w = f64(np.asarray(w, np.float32).astype(ml_dtypes.bfloat16)).reshape(k // 32, 32, n)
    amax = np.abs(w).max(1)
    if fmt == "e4m3":
        byte = np.frexp(amax)[1] - 1 + 127 - 7
    else:
        mant, ex = np.frexp(amax / 6.0)
        byte = np.where(mant > 0.5, ex, ex - 1) + 127
    byte = np.clip(np.where(amax > 0, byte, 1), 1, 254)
    scaled = (w * np.exp2(127.0 - byte)[:, None, :]).reshape(k, n).astype(np.float32)
    by_word = np.ascontiguousarray(scaled.reshape(k // 512, 128, 4, n).transpose(0, 1, 3, 2))
    if fmt == "e4m3":
        words = by_word.astype(ml_dtypes.float8_e4m3fn).view(np.uint8)
    else:
        c = by_word.astype(ml_dtypes.float4_e2m1fn).view(np.uint8) & 0xF
        words = (c[..., 0::2] | (c[..., 1::2] << 4)).reshape(k // 512, 128, 2 * n)
    return np.ascontiguousarray(words), np.ascontiguousarray(byte.astype(np.uint8).reshape(k // 512, 16, n))


def unpack_weight(words, scales, fmt):
    g, _, n = scales.shape
    words = np.ascontiguousarray(words).reshape(g, 128, n, -1)
    if fmt == "e4m3":
        vals = words.view(ml_dtypes.float8_e4m3fn).astype(np.float64)
    else:
        nib = np.empty((g, 128, n, 4), np.uint8)
        nib[..., 0::2] = words & 0xF
        nib[..., 1::2] = words >> 4
        vals = E2M1[nib]
    vals = vals * np.repeat(np.exp2(scales.astype(np.float64) - 127.0), 8, axis=1)[..., None]
    return vals.transpose(0, 1, 3, 2).reshape(g * 512, n)


def bf(x):
    return np.asarray(x, np.float32).astype(ml_dtypes.bfloat16)


def planes(Y):
    r, m = Y.shape
    b = f64(bf(Y)).reshape(r // 32, 32, m)
    amax = np.abs(b).max(1)
    byte = np.clip(np.where(amax > 0, np.frexp(amax)[1] - 1 + 127 - 7, 1), 1, 254)
    codes = (b * np.exp2(127.0 - byte)[:, None, :]).reshape(r, m).astype(np.float32).astype(ml_dtypes.float8_e4m3fn).view(np.uint8)
    words = codes.reshape(r // 512, 128, 4, m).transpose(0, 1, 3, 2)
    return np.ascontiguousarray(words), np.ascontiguousarray(byte.astype(np.uint8).reshape(r // 512, 16, m))


K, T, S, J, N = 1024, 1024, 512, 512, 512


def setup_inputs():
    n = np.random.standard_normal
    idx = np.stack([np.random.permutation(T)[:J] for _ in range(8)])
    idx2 = np.random.randint(0, S, J)
    fk = mx_kscale(K)
    wp = pack_weight(n((K, N)) * 1 / np.sqrt(K) * fk[:, None], "e4m3")
    return {
        "xf": (n((K, T))).astype(np.float32),
        "tb": (n((K, S))).astype(np.float32),
        "fk": (np.random.uniform(0.5, 2.0, (K, 1)) / fk[:, None]).astype(np.float32),
        "w_words": wp[0],
        "w_scales": wp[1],
        "rw": (np.random.uniform(0.5, 2.0, (1, J))).astype(np.float32),
        "offs": striped8(idx),
        "offs2": striped(idx2),
    }


def reference(xf, tb, fk, w_words, w_scales, rw, offs, offs2):
    idx = unstriped8(offs)
    idx2 = unstriped(offs2)
    wu = unpack_weight(w_words, w_scales, "e4m3")
    u = pick8(f64(xf), idx, 64) * f64(tb)[:, idx2] * f64(fk)
    uq = mxq(u, 0, "e4m3")
    p = wu.T @ uq
    y = p * f64(rw)
    words, scales = planes(y)
    return y, words, scales

@@ -1,0 +1,195 @@
+from contextlib import ExitStack
+
+import concourse.mybir as mybir
+from concourse.masks import make_identity
+
+K, T, S, J, N = 1024, 1024, 512, 512, 512
+P, PACK = 128, 4
+PASSES = K // (P * PACK)
+SPARE = 192
+FLOPS = 2 * K * N * J
+
+F32 = mybir.dt.float32
+BF16 = mybir.dt.bfloat16
+I32 = mybir.dt.int32
+U32 = mybir.dt.uint32
+U16 = mybir.dt.uint16
+U8 = mybir.dt.uint8
+FP8X4 = mybir.dt.float8_e4m3fn_x4
+COPY = mybir.ActivationFunctionType.Copy
+MULT = mybir.AluOpType.mult
+
+
+def tile_moe_expert_heads_times_key_pl_kernel(tc, xf, tb, fk, w_words, w_scales, rw, offs, offs2, out_0, out_1, out_2):
+    nc = tc.nc
+    with ExitStack() as ctx:
+        keep = ctx.enter_context(tc.tile_pool(name="keep", bufs=1))
+        psum = ctx.enter_context(tc.psum_pool(name="psum", bufs=1))
+        planes = PASSES * PACK
+
+        x_list = keep.tile([P, J // 16], U16, name="x_list")
+        key_list = keep.tile([P, J // 16], U16, name="key_list")
+        keys = keep.tile([P, planes * S + SPARE], F32, name="keys")
+        tokens = [keep.tile([P, T], F32, name="tokens%d" % i) for i in range(planes)]
+        factor = keep.tile([P, PASSES, PACK], F32, name="factor")
+        weight = keep.tile([P, J // P], F32, name="weight")
+        w_codes = keep.tile([P, PASSES, N], U32, name="w_codes", align_bytes=64)
+        w_plane = keep.tile([P, PASSES, N], U8, name="w_plane", align_bytes=64)
+        ident = keep.tile([P, P], F32, name="ident")
+
+        x_rows = xf.rearrange("(g p t) c -> g t p c", g=PASSES, t=PACK)
+        key_rows = tb.rearrange("(g p t) c -> g t p c", g=PASSES, t=PACK)
+
+        def key_start(i):
+            return (planes - 1 - i) * S
+
+        nc.vector.memset(keys[:, planes * S :], 0.0)
+        nc.vector.memset(w_plane[:].rearrange("p g n -> p (g n)").bitcast(I32), 0)
+        make_identity(nc, ident[:])
+
+        def load_keys(i):
+            nc.sync.dma_start(out=keys[:, key_start(i) : key_start(i) + S], in_=key_rows[i // PACK, i % PACK])
+
+        def load_tokens(i):
+            nc.sync.dma_start(out=tokens[i][:], in_=x_rows[i // PACK, i % PACK])
+
+        load_keys(0)
+        nc.sync.dma_start(key_list[:], offs2)
+        nc.scalar.dma_start(out=factor[:], in_=fk.rearrange("(g p t) o -> p g (t o)", g=PASSES, t=PACK))
+        load_keys(1)
+        nc.sync.dma_start(x_list[:], offs)
+        for i in range(planes):
+            load_tokens(i)
+            if i + 2 < planes:
+                load_keys(i + 2)
+        for g in range(PASSES):
+            nc.sync.dma_start(out=w_codes[:, g, :].bitcast(I32), in_=w_words[g].rearrange("p n t -> p (n t)").bitcast(I32))
+        scale_rows = w_scales.bitcast(I32).rearrange("g (q r) c -> r q g c", r=4)
+        for r in range(4):
+            nc.sync.dma_start(out=w_plane[r:P:32, :, :].bitcast(I32), in_=scale_rows[r])
+        with nc.allow_non_contiguous_dma(reason="one router weight a partition"):
+            nc.sync.dma_start(out=weight[:], in_=rw.rearrange("o (c p) -> p (o c)", p=P))
+
+        u_codes = [keep.tile([P, J], U32, name="u_codes%d" % g, align_bytes=64) for g in range(PASSES)]
+        u_plane = [keep.tile([P, J], U8, name="u_plane%d" % g, align_bytes=64) for g in range(PASSES)]
+        y_codes = keep.tile([P, J], U32, name="y_codes", align_bytes=64)
+        y_plane = keep.tile([P, J], U8, name="y_plane", align_bytes=64)
+        sums = [psum.tile([P, N], F32, name="sums%d" % c) for c in range(J // P)]
+        turned = [psum.tile([P, PACK, P], F32, name="turned%d" % c) for c in range(J // P)]
+
+        picked = {}
+        scaled = {}
+
+        def gather_keys(i):
+            picked[i] = keep.tile([P, J], F32, name="picked%d" % i)
+            window = keys[:, key_start(i) : key_start(i) + S + SPARE]
+            nc.vector.tensor_copy(picked[i][:], window.indirect(key_list[:]))
+
+        def scale_keys(i, lo, hi, tag):
+            scaled[i, lo] = keep.tile([P, hi - lo], F32, name="scaled", tag=tag, align_bytes=64)
+            nc.scalar.activation(scaled[i, lo][:], picked[i][:, lo:hi], COPY, scale=factor[:, i // PACK, i % PACK : i % PACK + 1])
+
+        def gather_tokens(u, i, lo, hi, other):
+            nc.vector.tensor_tensor(u[:, i % PACK, :], tokens[i][:].indirect(x_list[:, lo // 16 : hi // 16]), other, MULT)
+
+        def interleave(u, tag, copy=nc.scalar.copy):
+            width = u.shape[2]
+            grouped = keep.tile([P, width, PACK], BF16, name="grouped", tag=tag, align_bytes=64)
+            copy(grouped[:].rearrange("p (c i) t -> p c t i", i=4), u[:].rearrange("p t (c i) -> p c t i", i=4))
+            return grouped
+
+        def quantize_u(grouped, g, lo, hi):
+            nc.vector.quantize_mx(out=u_codes[g][:, lo:hi].bitcast(FP8X4), scales=u_plane[g][:, lo:hi],
+                                  in_=grouped[:].rearrange("p c t -> p (c t)"))
+
+        def multiply(c, g):
+            cols = slice(c * P, (c + 1) * P)
+            nc.tensor.matmul_mx(out=sums[c][:], lhsT=u_codes[g][:, cols].bitcast(FP8X4), lhsT_scale=u_plane[g][:, cols],
+                                rhs=w_codes[:, g, :].bitcast(FP8X4), rhs_scale=w_plane[:, g, :],
+                                start=(g == 0), stop=(g == PASSES - 1))
+
+        def weigh_and_turn(c):
+            y_t = keep.tile([P, PACK, P], F32, name="y_t%d" % c)
+            nc.scalar.activation(y_t[:], sums[c][:].rearrange("j (p t) -> j t p", t=PACK), COPY, scale=weight[:, c : c + 1])
+            for t in range(PACK):
+                nc.tensor.transpose(turned[c][:, t, :], y_t[:, t, :], ident[:])
+
+        y_rows = out_0.rearrange("(p t) j -> p t j", t=PACK)
+        word_rows = out_1[0].rearrange("p j t -> p (j t)").bitcast(I32)
+
+        def copy_out(y, c, lo, copy):
+            copy(y[:, :, c * P - lo : (c + 1) * P - lo], turned[c][:])
+
+        def hand_out(y, lo, hi):
+            cols = slice(lo, hi)
+            nc.sync.dma_start(out=y_rows[:, :, cols], in_=y[:])
+            grouped = keep.tile([P, hi - lo, PACK], BF16, name="y_grouped%d" % lo, align_bytes=64)
+            nc.vector.tensor_copy(grouped[:].rearrange("p (c i) t -> p c t i", i=4), y[:].rearrange("p t (c i) -> p c t i", i=4))
+            nc.vector.quantize_mx(out=y_codes[:, cols].bitcast(FP8X4), scales=y_plane[:, cols],
+                                  in_=grouped[:].rearrange("p c t -> p (c t)"))
+
+        u0 = keep.tile([P, PACK, J], F32, name="u0")
+        gather_keys(0)
+        scale_keys(0, 0, J, "scaled0")
+        for i in range(PACK):
+            gather_keys(i + 1)
+            scale_keys(i + 1, 0, J, "scaled%d" % (i + 1))
+            gather_tokens(u0, i, 0, J, scaled[i, 0][:])
+        grouped0 = interleave(u0, "grouped0")
+        gather_keys(5)
+        scale_keys(5, 0, J, "scaled5")
+        gather_keys(6)
+        scale_keys(6, 0, J, "scaled6")
+        quantize_u(grouped0, 0, 0, J)
+        for c in range(J // P):
+            multiply(c, 0)
+        gather_keys(7)
+        scale_keys(7, 0, 256, "pin_b")
+        scale_keys(7, 256, J, "scaled7")
+
+        def other(i, lo, hi):
+            if i < 7:
+                return scaled[i, 0][:, lo:hi]
+            if lo == 0:
+                return scaled[7, 0][:]
+            return scaled[7, 256][:, lo - 256 : hi - 256]
+
+        def gather_chunk(lo, hi, tag):
+            u = keep.tile([P, PACK, hi - lo], F32, name="u", tag=tag, align_bytes=64)
+            for i in range(PACK, planes):
+                gather_tokens(u, i, lo, hi, other(i, lo, hi))
+            return u
+
+        ua = gather_chunk(0, 256, "ua")
+        grouped_a = interleave(ua, "pin_c")
+        ub = gather_chunk(256, 384, "pin_b")
+        grouped_b = interleave(ub, "grouped_b")
+        quantize_u(grouped_a, 1, 0, 256)
+        multiply(0, 1)
+        multiply(1, 1)
+        quantize_u(grouped_b, 1, 256, 384)
+        multiply(2, 1)
+        weigh_and_turn(0)
+        weigh_and_turn(1)
+        uc = gather_chunk(384, 512, "pin_c")
+        grouped_c = interleave(uc, "grouped_c", nc.vector.tensor_copy)
+        quantize_u(grouped_c, 1, 384, 512)
+        multiply(3, 1)
+        weigh_and_turn(2)
+        ya = keep.tile([P, PACK, 256], F32, name="ya")
+        yb = keep.tile([P, PACK, P], F32, name="yb")
+        yc = keep.tile([P, PACK, P], F32, name="yc")
+        copy_out(ya, 0, 0, nc.scalar.copy)
+        weigh_and_turn(3)
+        copy_out(ya, 1, 0, nc.vector.tensor_copy)
+        hand_out(ya, 0, 256)
+        copy_out(yb, 2, 256, nc.scalar.copy)
+        hand_out(yb, 256, 384)
+        copy_out(yc, 3, 384, nc.scalar.copy)
+        hand_out(yc, 384, 512)
+        nc.sync.dma_start(out=word_rows[:, 0:384], in_=y_codes[:, 0:384].bitcast(I32))
+        nc.scalar.dma_start(out=word_rows[:, 384:512], in_=y_codes[:, 384:512].bitcast(I32))
+        scale_out = out_2[0].bitcast(I32).rearrange("(q r) c -> r q c", r=4)
+        for r in range(4):
+            queue = nc.scalar if r % 2 else nc.sync
+            queue.dma_start(out=scale_out[r], in_=y_plane[r:P:32, :].bitcast(I32))

@@ -57,25 +57,26 @@ def tile_moe_expert_heads_times_key_pl_kernel(tc, xf, tb, fk, w_words, w_scales,
         nc.sync.dma_start(key_list[:], offs2)
         nc.scalar.dma_start(out=factor[:], in_=fk.rearrange("(g p t) o -> p g (t o)", g=PASSES, t=PACK))
         load_keys(1)
+        load_keys(2)
         nc.sync.dma_start(x_list[:], offs)
         for i in range(planes):
             load_tokens(i)
-            if i + 2 < planes:
-                load_keys(i + 2)
+            if i + 3 < planes:
+                load_keys(i + 3)
+            if i == PACK:
+                with nc.allow_non_contiguous_dma(reason="one router weight a partition"):
+                    nc.sync.dma_start(out=weight[:], in_=rw.rearrange("o (c p) -> p (o c)", p=P))
         for g in range(PASSES):
             nc.sync.dma_start(out=w_codes[:, g, :].bitcast(I32), in_=w_words[g].rearrange("p n t -> p (n t)").bitcast(I32))
         scale_rows = w_scales.bitcast(I32).rearrange("g (q r) c -> r q g c", r=4)
         for r in range(4):
             nc.sync.dma_start(out=w_plane[r:P:32, :, :].bitcast(I32), in_=scale_rows[r])
-        with nc.allow_non_contiguous_dma(reason="one router weight a partition"):
-            nc.sync.dma_start(out=weight[:], in_=rw.rearrange("o (c p) -> p (o c)", p=P))
 
         u_codes = [keep.tile([P, J], U32, name="u_codes%d" % g, align_bytes=64) for g in range(PASSES)]
         u_plane = [keep.tile([P, J], U8, name="u_plane%d" % g, align_bytes=64) for g in range(PASSES)]
         y_codes = keep.tile([P, J], U32, name="y_codes", align_bytes=64)
         y_plane = keep.tile([P, J], U8, name="y_plane", align_bytes=64)
-        sums = [psum.tile([P, N], F32, name="sums%d" % c) for c in range(J // P)]
-        turned = [psum.tile([P, PACK, P], F32, name="turned%d" % c) for c in range(J // P)]
+        sums = {}
 
         picked = {}
         scaled = {}
@@ -108,44 +109,48 @@ def tile_moe_expert_heads_times_key_pl_kernel(tc, xf, tb, fk, w_words, w_scales,
                                 rhs=w_codes[:, g, :].bitcast(FP8X4), rhs_scale=w_plane[:, g, :],
                                 start=(g == 0), stop=(g == PASSES - 1))
 
-        def weigh_and_turn(c):
-            y_t = keep.tile([P, PACK, P], F32, name="y_t%d" % c)
-            nc.scalar.activation(y_t[:], sums[c][:].rearrange("j (p t) -> j t p", t=PACK), COPY, scale=weight[:, c : c + 1])
-            for t in range(PACK):
-                nc.tensor.transpose(turned[c][:, t, :], y_t[:, t, :], ident[:])
+        def weigh_and_turn(c, t0, t1):
+            y_t = keep.tile([P, t1 - t0, P], F32, name="y_t%d_%d" % (c, t0))
+            nc.scalar.activation(y_t[:], sums[c][:].rearrange("j (p t) -> j t p", t=PACK)[:, t0:t1, :], COPY, scale=weight[:, c : c + 1])
+            turned = psum.tile([P, t1 - t0, P], F32, name="turned%d_%d" % (c, t0))
+            for t in range(t1 - t0):
+                nc.tensor.transpose(turned[:, t, :], y_t[:, t, :], ident[:])
+            return turned
 
         y_rows = out_0.rearrange("(p t) j -> p t j", t=PACK)
         word_rows = out_1[0].rearrange("p j t -> p (j t)").bitcast(I32)
 
-        def copy_out(y, c, lo, copy):
-            copy(y[:, :, c * P - lo : (c + 1) * P - lo], turned[c][:])
+        def copy_out(c, turned):
+            y = keep.tile([P, PACK, P], F32, name="y%d" % c)
+            nc.scalar.copy(y[:], turned[:])
+            nc.sync.dma_start(out=y_rows[:, :, c * P : (c + 1) * P], in_=y[:])
+            return y
 
-        def hand_out(y, lo, hi):
-            cols = slice(lo, hi)
-            nc.sync.dma_start(out=y_rows[:, :, cols], in_=y[:])
-            grouped = keep.tile([P, hi - lo, PACK], BF16, name="y_grouped%d" % lo, align_bytes=64)
-            nc.vector.tensor_copy(grouped[:].rearrange("p (c i) t -> p c t i", i=4), y[:].rearrange("p t (c i) -> p c t i", i=4))
-            nc.vector.quantize_mx(out=y_codes[:, cols].bitcast(FP8X4), scales=y_plane[:, cols],
-                                  in_=grouped[:].rearrange("p c t -> p (c t)"))
+        def weave_y(grouped, y):
+            nc.vector.tensor_copy(grouped.rearrange("p (c i) t -> p c t i", i=4), y[:].rearrange("p t (c i) -> p c t i", i=4))
+
+        def quantize_y(grouped, lo, hi):
+            nc.vector.quantize_mx(out=y_codes[:, lo:hi].bitcast(FP8X4), scales=y_plane[:, lo:hi],
+                                  in_=grouped[:, lo:hi, :].rearrange("p c t -> p (c t)"))
 
         u0 = keep.tile([P, PACK, J], F32, name="u0")
-        gather_keys(0)
-        scale_keys(0, 0, J, "scaled0")
+        for i in range(2):
+            gather_keys(i)
+            scale_keys(i, 0, J, "scaled%d" % i)
         for i in range(PACK):
-            gather_keys(i + 1)
-            scale_keys(i + 1, 0, J, "scaled%d" % (i + 1))
+            gather_keys(i + 2)
+            scale_keys(i + 2, 0, J, "scaled%d" % (i + 2))
             gather_tokens(u0, i, 0, J, scaled[i, 0][:])
         grouped0 = interleave(u0, "grouped0")
-        gather_keys(5)
-        scale_keys(5, 0, J, "scaled5")
         gather_keys(6)
         scale_keys(6, 0, J, "scaled6")
-        quantize_u(grouped0, 0, 0, J)
-        for c in range(J // P):
-            multiply(c, 0)
         gather_keys(7)
         scale_keys(7, 0, 256, "pin_b")
         scale_keys(7, 256, J, "scaled7")
+        quantize_u(grouped0, 0, 0, J)
+        for c in range(3):
+            sums[c] = psum.tile([P, N], F32, name="sums", tag="sums%d" % c)
+            multiply(c, 0)
 
         def other(i, lo, hi):
             if i < 7:
@@ -169,26 +174,34 @@ def tile_moe_expert_heads_times_key_pl_kernel(tc, xf, tb, fk, w_words, w_scales,
         multiply(1, 1)
         quantize_u(grouped_b, 1, 256, 384)
         multiply(2, 1)
-        weigh_and_turn(0)
-        weigh_and_turn(1)
+        turned0 = weigh_and_turn(0, 0, PACK)
+        turned1 = weigh_and_turn(1, 0, PACK)
+        sums[3] = psum.tile([P, N], F32, name="sums", tag="sums1")
+        multiply(3, 0)
         uc = gather_chunk(384, 512, "pin_c")
         grouped_c = interleave(uc, "grouped_c", nc.vector.tensor_copy)
+
         quantize_u(grouped_c, 1, 384, 512)
+        turned2 = weigh_and_turn(2, 0, PACK)
         multiply(3, 1)
-        weigh_and_turn(2)
-        ya = keep.tile([P, PACK, 256], F32, name="ya")
-        yb = keep.tile([P, PACK, P], F32, name="yb")
-        yc = keep.tile([P, PACK, P], F32, name="yc")
-        copy_out(ya, 0, 0, nc.scalar.copy)
-        weigh_and_turn(3)
-        copy_out(ya, 1, 0, nc.vector.tensor_copy)
-        hand_out(ya, 0, 256)
-        copy_out(yb, 2, 256, nc.scalar.copy)
-        hand_out(yb, 256, 384)
-        copy_out(yc, 3, 384, nc.scalar.copy)
-        hand_out(yc, 384, 512)
-        nc.sync.dma_start(out=word_rows[:, 0:384], in_=y_codes[:, 0:384].bitcast(I32))
-        nc.scalar.dma_start(out=word_rows[:, 384:512], in_=y_codes[:, 384:512].bitcast(I32))
+        y_grouped = keep.tile([P, J, PACK], BF16, name="y_grouped", align_bytes=64)
+        y0 = copy_out(0, turned0)
+        weave_y(y_grouped[:, 0:128, :], y0)
+        y1 = copy_out(1, turned1)
+        weave_y(y_grouped[:, 128:256, :], y1)
+        turned3 = [weigh_and_turn(3, 0, 2), weigh_and_turn(3, 2, PACK)]
+        quantize_y(y_grouped, 0, 256)
+        nc.sync.dma_start(out=word_rows[:, 0:256], in_=y_codes[:, 0:256].bitcast(I32))
+        y2 = copy_out(2, turned2)
+        y3 = keep.tile([P, PACK, P], F32, name="y3")
+        nc.vector.tensor_copy(y3[:, 0:2, :], turned3[0][:])
+        nc.scalar.copy(y3[:, 2:PACK, :], turned3[1][:])
+        nc.scalar.dma_start(out=y_rows[:, :, 384:512], in_=y3[:])
+        weave_y(y_grouped[:, 256:384, :], y2)
+        weave_y(y_grouped[:, 384:512, :], y3)
+        quantize_y(y_grouped, 256, 384)
+        quantize_y(y_grouped, 384, 512)
+        nc.sync.dma_start(out=word_rows[:, 256:512], in_=y_codes[:, 256:512].bitcast(I32))
         scale_out = out_2[0].bitcast(I32).rearrange("(q r) c -> r q c", r=4)
         for r in range(4):
             queue = nc.scalar if r % 2 else nc.sync

from contextlib import ExitStack

import concourse.mybir as mybir
from concourse.masks import make_identity

K, T, S, J, N = 1024, 1024, 512, 512, 512
P, PACK = 128, 4
PASSES = K // (P * PACK)
SPARE = 192
FLOPS = 2 * K * N * J

F32 = mybir.dt.float32
BF16 = mybir.dt.bfloat16
I32 = mybir.dt.int32
U32 = mybir.dt.uint32
U16 = mybir.dt.uint16
U8 = mybir.dt.uint8
FP8X4 = mybir.dt.float8_e4m3fn_x4
COPY = mybir.ActivationFunctionType.Copy
MULT = mybir.AluOpType.mult


def tile_moe_expert_heads_times_key_pl_kernel(tc, xf, tb, fk, w_words, w_scales, rw, offs, offs2, out_0, out_1, out_2):
    nc = tc.nc
    with ExitStack() as ctx:
        keep = ctx.enter_context(tc.tile_pool(name="keep", bufs=1))
        psum = ctx.enter_context(tc.psum_pool(name="psum", bufs=1))
        planes = PASSES * PACK

        x_list = keep.tile([P, J // 16], U16, name="x_list")
        key_list = keep.tile([P, J // 16], U16, name="key_list")
        keys = keep.tile([P, planes * S + SPARE], F32, name="keys")
        tokens = [keep.tile([P, T], F32, name="tokens%d" % i) for i in range(planes)]
        factor = keep.tile([P, PASSES, PACK], F32, name="factor")
        weight = keep.tile([P, J // P], F32, name="weight")
        w_codes = keep.tile([P, PASSES, N], U32, name="w_codes", align_bytes=64)
        w_plane = keep.tile([P, PASSES, N], U8, name="w_plane", align_bytes=64)
        ident = keep.tile([P, P], F32, name="ident")

        x_rows = xf.rearrange("(g p t) c -> g t p c", g=PASSES, t=PACK)
        key_rows = tb.rearrange("(g p t) c -> g t p c", g=PASSES, t=PACK)

        def key_start(i):
            return (planes - 1 - i) * S

        nc.vector.memset(keys[:, planes * S :], 0.0)
        nc.vector.memset(w_plane[:].rearrange("p g n -> p (g n)").bitcast(I32), 0)
        make_identity(nc, ident[:])

        def load_keys(i):
            nc.sync.dma_start(out=keys[:, key_start(i) : key_start(i) + S], in_=key_rows[i // PACK, i % PACK])

        def load_tokens(i):
            nc.sync.dma_start(out=tokens[i][:], in_=x_rows[i // PACK, i % PACK])

        load_keys(0)
        nc.sync.dma_start(key_list[:], offs2)
        nc.scalar.dma_start(out=factor[:], in_=fk.rearrange("(g p t) o -> p g (t o)", g=PASSES, t=PACK))
        load_keys(1)
        load_keys(2)
        nc.sync.dma_start(x_list[:], offs)
        for i in range(planes):
            load_tokens(i)
            if i + 3 < planes:
                load_keys(i + 3)
            if i == PACK:
                with nc.allow_non_contiguous_dma(reason="one router weight a partition"):
                    nc.sync.dma_start(out=weight[:], in_=rw.rearrange("o (c p) -> p (o c)", p=P))
        for g in range(PASSES):
            nc.sync.dma_start(out=w_codes[:, g, :].bitcast(I32), in_=w_words[g].rearrange("p n t -> p (n t)").bitcast(I32))
        scale_rows = w_scales.bitcast(I32).rearrange("g (q r) c -> r q g c", r=4)
        for r in range(4):
            nc.sync.dma_start(out=w_plane[r:P:32, :, :].bitcast(I32), in_=scale_rows[r])

        u_codes = [keep.tile([P, J], U32, name="u_codes%d" % g, align_bytes=64) for g in range(PASSES)]
        u_plane = [keep.tile([P, J], U8, name="u_plane%d" % g, align_bytes=64) for g in range(PASSES)]
        y_codes = keep.tile([P, J], U32, name="y_codes", align_bytes=64)
        y_plane = keep.tile([P, J], U8, name="y_plane", align_bytes=64)
        sums = {}

        picked = {}
        scaled = {}

        def gather_keys(i):
            picked[i] = keep.tile([P, J], F32, name="picked%d" % i)
            window = keys[:, key_start(i) : key_start(i) + S + SPARE]
            nc.vector.tensor_copy(picked[i][:], window.indirect(key_list[:]))

        def scale_keys(i, lo, hi, tag):
            scaled[i, lo] = keep.tile([P, hi - lo], F32, name="scaled", tag=tag, align_bytes=64)
            nc.scalar.activation(scaled[i, lo][:], picked[i][:, lo:hi], COPY, scale=factor[:, i // PACK, i % PACK : i % PACK + 1])

        def gather_tokens(u, i, lo, hi, other):
            nc.vector.tensor_tensor(u[:, i % PACK, :], tokens[i][:].indirect(x_list[:, lo // 16 : hi // 16]), other, MULT)

        def interleave(u, tag, copy=nc.scalar.copy):
            width = u.shape[2]
            grouped = keep.tile([P, width, PACK], BF16, name="grouped", tag=tag, align_bytes=64)
            copy(grouped[:].rearrange("p (c i) t -> p c t i", i=4), u[:].rearrange("p t (c i) -> p c t i", i=4))
            return grouped

        def quantize_u(grouped, g, lo, hi):
            nc.vector.quantize_mx(out=u_codes[g][:, lo:hi].bitcast(FP8X4), scales=u_plane[g][:, lo:hi],
                                  in_=grouped[:].rearrange("p c t -> p (c t)"))

        def multiply(c, g):
            cols = slice(c * P, (c + 1) * P)
            nc.tensor.matmul_mx(out=sums[c][:], lhsT=u_codes[g][:, cols].bitcast(FP8X4), lhsT_scale=u_plane[g][:, cols],
                                rhs=w_codes[:, g, :].bitcast(FP8X4), rhs_scale=w_plane[:, g, :],
                                start=(g == 0), stop=(g == PASSES - 1))

        def weigh_and_turn(c, t0, t1):
            y_t = keep.tile([P, t1 - t0, P], F32, name="y_t%d_%d" % (c, t0))
            nc.scalar.activation(y_t[:], sums[c][:].rearrange("j (p t) -> j t p", t=PACK)[:, t0:t1, :], COPY, scale=weight[:, c : c + 1])
            turned = psum.tile([P, t1 - t0, P], F32, name="turned%d_%d" % (c, t0))
            for t in range(t1 - t0):
                nc.tensor.transpose(turned[:, t, :], y_t[:, t, :], ident[:])
            return turned

        y_rows = out_0.rearrange("(p t) j -> p t j", t=PACK)
        word_rows = out_1[0].rearrange("p j t -> p (j t)").bitcast(I32)

        def copy_out(c, turned):
            y = keep.tile([P, PACK, P], F32, name="y%d" % c)
            nc.scalar.copy(y[:], turned[:])
            nc.sync.dma_start(out=y_rows[:, :, c * P : (c + 1) * P], in_=y[:])
            return y

        def weave_y(grouped, y):
            nc.vector.tensor_copy(grouped.rearrange("p (c i) t -> p c t i", i=4), y[:].rearrange("p t (c i) -> p c t i", i=4))

        def quantize_y(grouped, lo, hi):
            nc.vector.quantize_mx(out=y_codes[:, lo:hi].bitcast(FP8X4), scales=y_plane[:, lo:hi],
                                  in_=grouped[:, lo:hi, :].rearrange("p c t -> p (c t)"))

        u0 = keep.tile([P, PACK, J], F32, name="u0")
        for i in range(2):
            gather_keys(i)
            scale_keys(i, 0, J, "scaled%d" % i)
        for i in range(PACK):
            gather_keys(i + 2)
            scale_keys(i + 2, 0, J, "scaled%d" % (i + 2))
            gather_tokens(u0, i, 0, J, scaled[i, 0][:])
        grouped0 = interleave(u0, "grouped0")
        gather_keys(6)
        scale_keys(6, 0, J, "scaled6")
        gather_keys(7)
        scale_keys(7, 0, 256, "pin_b")
        scale_keys(7, 256, J, "scaled7")
        quantize_u(grouped0, 0, 0, J)
        for c in range(3):
            sums[c] = psum.tile([P, N], F32, name="sums", tag="sums%d" % c)
            multiply(c, 0)

        def other(i, lo, hi):
            if i < 7:
                return scaled[i, 0][:, lo:hi]
            if lo == 0:
                return scaled[7, 0][:]
            return scaled[7, 256][:, lo - 256 : hi - 256]

        def gather_chunk(lo, hi, tag):
            u = keep.tile([P, PACK, hi - lo], F32, name="u", tag=tag, align_bytes=64)
            for i in range(PACK, planes):
                gather_tokens(u, i, lo, hi, other(i, lo, hi))
            return u

        ua = gather_chunk(0, 256, "ua")
        grouped_a = interleave(ua, "pin_c")
        ub = gather_chunk(256, 384, "pin_b")
        grouped_b = interleave(ub, "grouped_b")
        quantize_u(grouped_a, 1, 0, 256)
        multiply(0, 1)
        multiply(1, 1)
        quantize_u(grouped_b, 1, 256, 384)
        multiply(2, 1)
        turned0 = weigh_and_turn(0, 0, PACK)
        turned1 = weigh_and_turn(1, 0, PACK)
        sums[3] = psum.tile([P, N], F32, name="sums", tag="sums1")
        multiply(3, 0)
        uc = gather_chunk(384, 512, "pin_c")
        grouped_c = interleave(uc, "grouped_c", nc.vector.tensor_copy)

        quantize_u(grouped_c, 1, 384, 512)
        turned2 = weigh_and_turn(2, 0, PACK)
        multiply(3, 1)
        y_grouped = keep.tile([P, J, PACK], BF16, name="y_grouped", align_bytes=64)
        y0 = copy_out(0, turned0)
        weave_y(y_grouped[:, 0:128, :], y0)
        y1 = copy_out(1, turned1)
        weave_y(y_grouped[:, 128:256, :], y1)
        turned3 = [weigh_and_turn(3, 0, 2), weigh_and_turn(3, 2, PACK)]
        quantize_y(y_grouped, 0, 256)
        nc.sync.dma_start(out=word_rows[:, 0:256], in_=y_codes[:, 0:256].bitcast(I32))
        y2 = copy_out(2, turned2)
        y3 = keep.tile([P, PACK, P], F32, name="y3")
        nc.vector.tensor_copy(y3[:, 0:2, :], turned3[0][:])
        nc.scalar.copy(y3[:, 2:PACK, :], turned3[1][:])
        nc.scalar.dma_start(out=y_rows[:, :, 384:512], in_=y3[:])
        weave_y(y_grouped[:, 256:384, :], y2)
        weave_y(y_grouped[:, 384:512, :], y3)
        quantize_y(y_grouped, 256, 384)
        quantize_y(y_grouped, 384, 512)
        nc.sync.dma_start(out=word_rows[:, 256:512], in_=y_codes[:, 256:512].bitcast(I32))
        scale_out = out_2[0].bitcast(I32).rearrange("(q r) c -> r q c", r=4)
        for r in range(4):
            queue = nc.scalar if r % 2 else nc.sync
            queue.dma_start(out=scale_out[r], in_=y_plane[r:P:32, :].bitcast(I32))
